import numpy as np
import ml_dtypes


def mxq(x, axis, fmt="e4m3"):
    dtype, down = {"e4m3": (ml_dtypes.float8_e4m3fn, 7), "e5m2": (ml_dtypes.float8_e5m2, 14)}[fmt]
    v = np.moveaxis(np.asarray(x, np.float32).astype(ml_dtypes.bfloat16).astype(np.float64), axis, -1)
    blocks = v.reshape(v.shape[:-1] + (-1, 32))
    amax = np.abs(blocks).max(-1, keepdims=True)
    byte = np.maximum(np.where(amax > 0, np.frexp(amax)[1] - 1 + 127, 0) - down, 1)
    scale = np.exp2(byte - 127.0)
    codes = (blocks / scale).astype(np.float32).astype(dtype).astype(np.float64)
    return np.moveaxis((codes * scale).reshape(v.shape), -1, axis)


WIDE = False


def mx_kscale(k):
    if not WIDE:
        return np.ones(k)
    levels = np.array([10, -10, 5, -5, 0])
    if k % 512:
        return np.exp2(np.random.permutation(np.resize(levels, k // 32))).repeat(32)
    a = np.empty((k // 512, 16))
    for p in range(k // 512):
        a[p, :8] = np.random.permutation(np.resize(levels, 8))
        for g in range(8):
            far = levels[np.abs(levels - a[p, g]) >= 10]
            a[p, g + 8] = far[np.random.randint(len(far))]
    return np.exp2(a.ravel()).repeat(32)


def f64(x):
    return np.asarray(x).astype(np.float64)


def striped8(idx):
    return np.concatenate([v.reshape(-1, 16).T for v in idx]).astype(np.uint16)


def unstriped8(offs):
    return np.stack([offs[16 * g:16 * g + 16].T.reshape(-1) for g in range(8)]).astype(np.int64)


E2M1 = np.array([0.0, 0.5, 1.0, 1.5, 2.0, 3.0, 4.0, 6.0, -0.0, -0.5, -1.0, -1.5, -2.0, -3.0, -4.0, -6.0])


def pack_weight(w, fmt):
    k, n = w.shape
    w = f64(np.asarray(w, np.float32).astype(ml_dtypes.bfloat16)).reshape(k // 32, 32, n)
    amax = np.abs(w).max(1)
    if fmt == "e4m3":
        byte = np.frexp(amax)[1] - 1 + 127 - 7
    else:
        mant, ex = np.frexp(amax / 6.0)
        byte = np.where(mant > 0.5, ex, ex - 1) + 127
    byte = np.clip(np.where(amax > 0, byte, 1), 1, 254)
    scaled = (w * np.exp2(127.0 - byte)[:, None, :]).reshape(k, n).astype(np.float32)
    by_word = np.ascontiguousarray(scaled.reshape(k // 512, 128, 4, n).transpose(0, 1, 3, 2))
    if fmt == "e4m3":
        words = by_word.astype(ml_dtypes.float8_e4m3fn).view(np.uint8)
    else:
        c = by_word.astype(ml_dtypes.float4_e2m1fn).view(np.uint8) & 0xF
        words = (c[..., 0::2] | (c[..., 1::2] << 4)).reshape(k // 512, 128, 2 * n)
    return np.ascontiguousarray(words), np.ascontiguousarray(byte.astype(np.uint8).reshape(k // 512, 16, n))


def unpack_weight(words, scales, fmt):
    g, _, n = scales.shape
    words = np.ascontiguousarray(words).reshape(g, 128, n, -1)
    if fmt == "e4m3":
        vals = words.view(ml_dtypes.float8_e4m3fn).astype(np.float64)
    else:
        nib = np.empty((g, 128, n, 4), np.uint8)
        nib[..., 0::2] = words & 0xF
        nib[..., 1::2] = words >> 4
        vals = E2M1[nib]
    vals = vals * np.repeat(np.exp2(scales.astype(np.float64) - 127.0), 8, axis=1)[..., None]
    return vals.transpose(0, 1, 3, 2).reshape(g * 512, n)


K, M, T, S = 2048, 512, 1024, 512


def setup_inputs():
    n = np.random.standard_normal
    s = mx_kscale(K)[:, None]
    p_w = pack_weight(n((K, M)) / np.sqrt(K) / s, "e2m1")
    return {
        "xT": (n((K, T)) * s).astype(np.float32),
        "w_words": p_w[0],
        "w_scales": p_w[1],
        "wgt": np.repeat(np.random.uniform(0.5, 2.0, (8, S)), 16, axis=0).astype(np.float32),
        "r": (n((512, 512))).astype(np.float32),
        "offs": striped8(np.stack([np.random.permutation(T)[:S] for _ in range(8)])),
    }


def reference(xT, w_words, w_scales, wgt, r, offs):
    idx = unstriped8(offs)
    group = np.arange(K) % 512 // 64
    xg = f64(wgt)[np.arange(K) // 4 % 128] * f64(xT)[np.arange(K)[:, None], idx[group]]
    xT_ = mxq(xg, 0, "e4m3")
    w_ = unpack_weight(w_words, w_scales, "e2m1")
    y = xT_.T @ w_
    return f64(r) + y

@@ -1,0 +1,150 @@
+from contextlib import ExitStack
+
+import concourse.mybir as mybir
+
+K, M, T, S = 2048, 512, 1024, 512
+FLOPS = 2 * K * M * S
+
+F32 = mybir.dt.float32
+BF16 = mybir.dt.bfloat16
+I32 = mybir.dt.int32
+U32 = mybir.dt.uint32
+U16 = mybir.dt.uint16
+U8 = mybir.dt.uint8
+E4M3X4 = mybir.dt.float8_e4m3fn_x4
+E2M1X4 = mybir.dt.float4_e2m1fn_x4
+MULT = mybir.AluOpType.mult
+ADD = mybir.AluOpType.add
+
+P = 128
+PACK = 4
+K_PASS = P * PACK
+PASSES = K // K_PASS
+TOK = 128
+TOK_TILES = S // TOK
+PER_COL = 16
+
+
+def tile_list_heads_tm_res_kernel(tc, xT, w_words, w_scales, wgt, r, offs, out):
+    nc = tc.nc
+    with ExitStack() as ctx:
+        lists = ctx.enter_context(tc.tile_pool(name="lists", bufs=1))
+        keep = ctx.enter_context(tc.tile_pool(name="keep", bufs=1))
+        psum = ctx.enter_context(tc.psum_pool(name="psum", bufs=1))
+
+        offsets = lists.tile([P, S // PER_COL], U16, name="offsets")
+        x = [[keep.tile([P, T], F32, name=f"x{a}_{i}") for i in range(PACK)] for a in range(PASSES)]
+        wg = [keep.tile([P, 256], F32, name=f"wg{h}") for h in range(2)]
+        picked = [keep.tile([P, PACK, S], F32, name=f"picked{a}", align_bytes=64) for a in range(PASSES)]
+        grouped = [keep.tile([P, S, PACK], BF16, name=f"grouped{a}", align_bytes=64) for a in range(PASSES)]
+        codes = [keep.tile([P, S], U32, name=f"codes{a}", align_bytes=64) for a in range(PASSES)]
+        scales = [keep.tile([P, S], U8, name=f"scales{a}", align_bytes=64) for a in range(PASSES)]
+        ww = keep.tile([P, PASSES, 2 * M], U8, name="ww", align_bytes=64)
+        ws = keep.tile([P, PASSES, M], U8, name="ws", align_bytes=64)
+        res = [keep.tile([P, M], F32, name=f"res{t}") for t in range(TOK_TILES)]
+        done = [keep.tile([P, M], F32, name=f"done{t}") for t in range(TOK_TILES)]
+        acc = [psum.tile([P, M], F32, name=f"acc{t}") for t in range(TOK_TILES)]
+
+        def load_x(a, i):
+            rows = xT[a * K_PASS : (a + 1) * K_PASS, :].rearrange("(p i) t -> p i t", i=PACK)
+            nc.sync.dma_start(out=x[a][i][:], in_=rows[:, i, :])
+
+        def gather(a, i, lo, hi):
+            half = lo // 256
+            nc.vector.tensor_tensor(
+                picked[a][:, i, lo:hi],
+                x[a][i][:].indirect(offsets[:, lo // PER_COL : hi // PER_COL]),
+                wg[half][:, lo - 256 * half : hi - 256 * half],
+                MULT,
+            )
+
+        def interleave(a, lo, hi):
+            nc.scalar.copy(
+                out=grouped[a][:, lo:hi, :],
+                in_=picked[a][:, :, lo:hi].rearrange("p i j -> p j i"),
+            )
+
+        def quantise(a, lo, hi):
+            nc.vector.quantize_mx(
+                out=codes[a][:, lo:hi].bitcast(E4M3X4),
+                scales=scales[a][:, lo:hi],
+                in_=grouped[a][:, lo:hi, :].rearrange("p j i -> p (j i)"),
+            )
+
+        def multiply(a, t):
+            cols = slice(t * TOK, (t + 1) * TOK)
+            nc.tensor.matmul_mx(
+                out=acc[t][:],
+                lhsT=codes[a][:, cols].bitcast(E4M3X4),
+                lhsT_scale=scales[a][:, cols],
+                rhs=ww[:, a, :].bitcast(E2M1X4),
+                rhs_scale=ws[:, a, :],
+                start=(a == 0),
+                stop=(a == PASSES - 1),
+            )
+
+        def finish(t):
+            rows = slice(t * TOK, (t + 1) * TOK)
+            nc.vector.tensor_tensor(done[t][:], acc[t][:], res[t][:], ADD)
+            nc.sync.dma_start(out=out[rows, :], in_=done[t][:])
+
+        nc.sync.dma_start(offsets[:], offs)
+        nc.scalar.dma_start(out=wg[0][:], in_=wgt[:, 0:256])
+        nc.vector.memset(ws[:].rearrange("p a n -> p (a n)").bitcast(I32), 0)
+        load_x(0, 0)
+        nc.sync.dma_start(out=wg[1][:], in_=wgt[:, 256:512])
+        for i in range(1, PACK):
+            load_x(0, i)
+        for i in range(PACK):
+            load_x(1, i)
+        nc.sync.dma_start(
+            out=ww[:].rearrange("p a n -> p (a n)").bitcast(I32).rearrange("p (a n) -> p a n", a=PASSES),
+            in_=w_words.rearrange("a p n -> p a n").bitcast(I32),
+        )
+        for q in range(4):
+            nc.scalar.dma_start(
+                out=ws[32 * q : 32 * q + 4, :, :].bitcast(I32),
+                in_=w_scales[:, 4 * q : 4 * q + 4, :].rearrange("a q n -> q a n").bitcast(I32),
+            )
+        for a in range(2, PASSES):
+            for i in range(PACK):
+                load_x(a, i)
+        for t in range(TOK_TILES):
+            nc.sync.dma_start(out=res[t][:], in_=r[t * TOK : (t + 1) * TOK, :])
+
+        last = PASSES - 1
+        for a in range(last):
+            for i in range(PACK):
+                gather(a, i, 0, 256)
+                gather(a, i, 256, 512)
+                if i == 1 and a > 0:
+                    quantise(a - 1, 0, S)
+                    for t in range(TOK_TILES):
+                        multiply(a - 1, t)
+            interleave(a, 0, 256)
+            interleave(a, 256, 512)
+
+        for i in range(PACK):
+            gather(last, i, 0, 256)
+            if i == 1:
+                quantise(last - 1, 0, S)
+                for t in range(TOK_TILES):
+                    multiply(last - 1, t)
+        interleave(last, 0, 256)
+        for i in range(PACK):
+            gather(last, i, 256, 384)
+        interleave(last, 256, 384)
+        quantise(last, 0, 256)
+        multiply(last, 0)
+        multiply(last, 1)
+        for i in range(PACK):
+            gather(last, i, 384, 512)
+        interleave(last, 384, 512)
+        quantise(last, 256, 384)
+        multiply(last, 2)
+        finish(0)
+        finish(1)
+        quantise(last, 384, 512)
+        multiply(last, 3)
+        finish(2)
+        finish(3)

@@ -91,6 +91,11 @@ def tile_list_heads_tm_res_kernel(tc, xT, w_words, w_scales, wgt, r, offs, out):
         nc.sync.dma_start(offsets[:], offs)
         nc.scalar.dma_start(out=wg[0][:], in_=wgt[:, 0:256])
         nc.vector.memset(ws[:].rearrange("p a n -> p (a n)").bitcast(I32), 0)
+        for q in range(4):
+            nc.scalar.dma_start(
+                out=ws[32 * q : 32 * q + 4, :, :].bitcast(I32),
+                in_=w_scales[:, 4 * q : 4 * q + 4, :].rearrange("a q n -> q a n").bitcast(I32),
+            )
         load_x(0, 0)
         nc.sync.dma_start(out=wg[1][:], in_=wgt[:, 256:512])
         for i in range(1, PACK):
@@ -101,11 +106,6 @@ def tile_list_heads_tm_res_kernel(tc, xT, w_words, w_scales, wgt, r, offs, out):
             out=ww[:].rearrange("p a n -> p (a n)").bitcast(I32).rearrange("p (a n) -> p a n", a=PASSES),
             in_=w_words.rearrange("a p n -> p a n").bitcast(I32),
         )
-        for q in range(4):
-            nc.scalar.dma_start(
-                out=ws[32 * q : 32 * q + 4, :, :].bitcast(I32),
-                in_=w_scales[:, 4 * q : 4 * q + 4, :].rearrange("a q n -> q a n").bitcast(I32),
-            )
         for a in range(2, PASSES):
             for i in range(PACK):
                 load_x(a, i)
@@ -124,27 +124,31 @@ def tile_list_heads_tm_res_kernel(tc, xT, w_words, w_scales, wgt, r, offs, out):
             interleave(a, 0, 256)
             interleave(a, 256, 512)
 
-        for i in range(PACK):
+        for i in range(PACK - 1):
             gather(last, i, 0, 256)
+            gather(last, i, 256, 384)
+            gather(last, i, 384, 512)
             if i == 1:
                 quantise(last - 1, 0, S)
                 for t in range(TOK_TILES):
                     multiply(last - 1, t)
+        gather(last, 3, 0, 256)
         interleave(last, 0, 256)
-        for i in range(PACK):
-            gather(last, i, 256, 384)
+        gather(last, 3, 384, 512)
+        gather(last, 3, 256, 384)
+        nc.vector.tensor_copy(
+            out=grouped[last][:, 384:512, :],
+            in_=picked[last][:, :, 384:512].rearrange("p i j -> p j i"),
+        )
         interleave(last, 256, 384)
         quantise(last, 0, 256)
         multiply(last, 0)
         multiply(last, 1)
-        for i in range(PACK):
-            gather(last, i, 384, 512)
-        interleave(last, 384, 512)
-        quantise(last, 256, 384)
-        multiply(last, 2)
-        finish(0)
-        finish(1)
         quantise(last, 384, 512)
         multiply(last, 3)
-        finish(2)
+        finish(0)
+        finish(1)
+        quantise(last, 256, 384)
+        multiply(last, 2)
         finish(3)
+        finish(2)

@@ -60,8 +60,8 @@ def tile_list_heads_tm_res_kernel(tc, xT, w_words, w_scales, wgt, r, offs, out):
 
         def interleave(a, lo, hi):
             nc.scalar.copy(
-                out=grouped[a][:, lo:hi, :],
-                in_=picked[a][:, :, lo:hi].rearrange("p i j -> p j i"),
+                out=grouped[a][:, lo:hi, :].rearrange("p (c l) i -> p c i l", l=4),
+                in_=picked[a][:, :, lo:hi].rearrange("p i (c l) -> p c i l", l=4),
             )
 
         def quantise(a, lo, hi):
@@ -117,7 +117,7 @@ def tile_list_heads_tm_res_kernel(tc, xT, w_words, w_scales, wgt, r, offs, out):
             for i in range(PACK):
                 gather(a, i, 0, 256)
                 gather(a, i, 256, 512)
-                if i == 1 and a > 0:
+                if i == 2 and a > 0:
                     quantise(a - 1, 0, S)
                     for t in range(TOK_TILES):
                         multiply(a - 1, t)
@@ -128,7 +128,7 @@ def tile_list_heads_tm_res_kernel(tc, xT, w_words, w_scales, wgt, r, offs, out):
             gather(last, i, 0, 256)
             gather(last, i, 256, 384)
             gather(last, i, 384, 512)
-            if i == 1:
+            if i == 2:
                 quantise(last - 1, 0, S)
                 for t in range(TOK_TILES):
                     multiply(last - 1, t)
@@ -137,8 +137,8 @@ def tile_list_heads_tm_res_kernel(tc, xT, w_words, w_scales, wgt, r, offs, out):
         gather(last, 3, 384, 512)
         gather(last, 3, 256, 384)
         nc.vector.tensor_copy(
-            out=grouped[last][:, 384:512, :],
-            in_=picked[last][:, :, 384:512].rearrange("p i j -> p j i"),
+            out=grouped[last][:, 384:512, :].rearrange("p (c l) i -> p c i l", l=4),
+            in_=picked[last][:, :, 384:512].rearrange("p i (c l) -> p c i l", l=4),
         )
         interleave(last, 256, 384)
         quantise(last, 0, 256)

@@ -33,14 +33,19 @@ def tile_list_heads_tm_res_kernel(tc, xT, w_words, w_scales, wgt, r, offs, out):
         psum = ctx.enter_context(tc.psum_pool(name="psum", bufs=1))
 
         offsets = lists.tile([P, S // PER_COL], U16, name="offsets")
-        x = [[keep.tile([P, T], F32, name=f"x{a}_{i}") for i in range(PACK)] for a in range(PASSES)]
+        x = [
+            [
+                keep.tile([P, T], F32, name=f"x{a}_{i}", tag="early" if (a, i) == (1, 2) else f"x{a}_{i}", align_bytes=64)
+                for i in range(PACK)
+            ]
+            for a in range(PASSES)
+        ]
         wg = [keep.tile([P, 256], F32, name=f"wg{h}") for h in range(2)]
         picked = [keep.tile([P, PACK, S], F32, name=f"picked{a}", align_bytes=64) for a in range(PASSES)]
         grouped = [keep.tile([P, S, PACK], BF16, name=f"grouped{a}", align_bytes=64) for a in range(PASSES)]
         codes = [keep.tile([P, S], U32, name=f"codes{a}", align_bytes=64) for a in range(PASSES)]
         scales = [keep.tile([P, S], U8, name=f"scales{a}", align_bytes=64) for a in range(PASSES)]
         ww = keep.tile([P, PASSES, 2 * M], U8, name="ww", align_bytes=64)
-        ws = keep.tile([P, PASSES, M], U8, name="ws", align_bytes=64)
         res = [keep.tile([P, M], F32, name=f"res{t}") for t in range(TOK_TILES)]
         done = [keep.tile([P, M], F32, name=f"done{t}") for t in range(TOK_TILES)]
         acc = [psum.tile([P, M], F32, name=f"acc{t}") for t in range(TOK_TILES)]
@@ -71,7 +76,7 @@ def tile_list_heads_tm_res_kernel(tc, xT, w_words, w_scales, wgt, r, offs, out):
                 in_=grouped[a][:, lo:hi, :].rearrange("p j i -> p (j i)"),
             )
 
-        def multiply(a, t):
+        def multiply(ws, a, t):
             cols = slice(t * TOK, (t + 1) * TOK)
             nc.tensor.matmul_mx(
                 out=acc[t][:],
@@ -90,65 +95,77 @@ def tile_list_heads_tm_res_kernel(tc, xT, w_words, w_scales, wgt, r, offs, out):
 
         nc.sync.dma_start(offsets[:], offs)
         nc.scalar.dma_start(out=wg[0][:], in_=wgt[:, 0:256])
-        nc.vector.memset(ws[:].rearrange("p a n -> p (a n)").bitcast(I32), 0)
-        for q in range(4):
-            nc.scalar.dma_start(
-                out=ws[32 * q : 32 * q + 4, :, :].bitcast(I32),
-                in_=w_scales[:, 4 * q : 4 * q + 4, :].rearrange("a q n -> q a n").bitcast(I32),
-            )
         load_x(0, 0)
         nc.sync.dma_start(out=wg[1][:], in_=wgt[:, 256:512])
         for i in range(1, PACK):
             load_x(0, i)
         for i in range(PACK):
             load_x(1, i)
+        for i in range(PACK):
+            load_x(2, i)
         nc.sync.dma_start(
             out=ww[:].rearrange("p a n -> p (a n)").bitcast(I32).rearrange("p (a n) -> p a n", a=PASSES),
             in_=w_words.rearrange("a p n -> p a n").bitcast(I32),
         )
-        for a in range(2, PASSES):
-            for i in range(PACK):
-                load_x(a, i)
+        for i in range(PACK):
+            load_x(3, i)
         for t in range(TOK_TILES):
             nc.sync.dma_start(out=res[t][:], in_=r[t * TOK : (t + 1) * TOK, :])
 
         last = PASSES - 1
+        ws = None
         for a in range(last):
             for i in range(PACK):
                 gather(a, i, 0, 256)
                 gather(a, i, 256, 512)
                 if i == 2 and a > 0:
                     quantise(a - 1, 0, S)
+                if i == 2 and a == 1:
+                    ws = keep.tile([P, PASSES, M], U8, name="ws", tag="early", align_bytes=64)
+                    nc.gpsimd.memset(ws[:].rearrange("p a n -> p (a n)").bitcast(I32), 0)
+                    for q in range(4):
+                        nc.scalar.dma_start(
+                            out=ws[32 * q : 32 * q + 4, :, :].bitcast(I32),
+                            in_=w_scales[:, 4 * q : 4 * q + 4, :].rearrange("a q n -> q a n").bitcast(I32),
+                        )
+                if i == 2 and a > 0:
                     for t in range(TOK_TILES):
-                        multiply(a - 1, t)
+                        multiply(ws, a - 1, t)
             interleave(a, 0, 256)
             interleave(a, 256, 512)
 
-        for i in range(PACK - 1):
-            gather(last, i, 0, 256)
-            gather(last, i, 256, 384)
-            gather(last, i, 384, 512)
-            if i == 2:
-                quantise(last - 1, 0, S)
-                for t in range(TOK_TILES):
-                    multiply(last - 1, t)
-        gather(last, 3, 0, 256)
-        interleave(last, 0, 256)
-        gather(last, 3, 384, 512)
+        gather(last, 0, 0, 256)
+        gather(last, 0, 256, 512)
+        gather(last, 1, 0, 256)
+        gather(last, 1, 256, 512)
+        quantise(last - 1, 0, 256)
+        multiply(ws, last - 1, 0)
+        multiply(ws, last - 1, 1)
+        gather(last, 2, 0, 256)
+        quantise(last - 1, 256, 512)
+        multiply(ws, last - 1, 2)
+        multiply(ws, last - 1, 3)
+        gather(last, 2, 256, 512)
+        gather(last, 3, 0, 128)
+        interleave(last, 0, 128)
+        gather(last, 3, 128, 256)
+        interleave(last, 128, 256)
         gather(last, 3, 256, 384)
+        interleave(last, 256, 384)
+        gather(last, 3, 384, 512)
+        quantise(last, 0, 128)
+        multiply(ws, last, 0)
         nc.vector.tensor_copy(
             out=grouped[last][:, 384:512, :].rearrange("p (c l) i -> p c i l", l=4),
             in_=picked[last][:, :, 384:512].rearrange("p i (c l) -> p c i l", l=4),
         )
-        interleave(last, 256, 384)
-        quantise(last, 0, 256)
-        multiply(last, 0)
-        multiply(last, 1)
-        quantise(last, 384, 512)
-        multiply(last, 3)
+        quantise(last, 128, 256)
+        multiply(ws, last, 1)
         finish(0)
-        finish(1)
         quantise(last, 256, 384)
-        multiply(last, 2)
-        finish(3)
+        multiply(ws, last, 2)
+        quantise(last, 384, 512)
+        multiply(ws, last, 3)
+        finish(1)
         finish(2)
+        finish(3)

@@ -35,7 +35,7 @@ def tile_list_heads_tm_res_kernel(tc, xT, w_words, w_scales, wgt, r, offs, out):
         offsets = lists.tile([P, S // PER_COL], U16, name="offsets")
         x = [
             [
-                keep.tile([P, T], F32, name=f"x{a}_{i}", tag="early" if (a, i) == (1, 2) else f"x{a}_{i}", align_bytes=64)
+                keep.tile([P, T], F32, name=f"x{a}_{i}", tag="early" if (a, i) == (0, 2) else f"x{a}_{i}", align_bytes=64)
                 for i in range(PACK)
             ]
             for a in range(PASSES)
@@ -101,14 +101,13 @@ def tile_list_heads_tm_res_kernel(tc, xT, w_words, w_scales, wgt, r, offs, out):
             load_x(0, i)
         for i in range(PACK):
             load_x(1, i)
-        for i in range(PACK):
-            load_x(2, i)
         nc.sync.dma_start(
             out=ww[:].rearrange("p a n -> p (a n)").bitcast(I32).rearrange("p (a n) -> p a n", a=PASSES),
             in_=w_words.rearrange("a p n -> p a n").bitcast(I32),
         )
-        for i in range(PACK):
-            load_x(3, i)
+        for a in range(2, PASSES):
+            for i in range(PACK):
+                load_x(a, i)
         for t in range(TOK_TILES):
             nc.sync.dma_start(out=res[t][:], in_=r[t * TOK : (t + 1) * TOK, :])
 
@@ -118,9 +117,7 @@ def tile_list_heads_tm_res_kernel(tc, xT, w_words, w_scales, wgt, r, offs, out):
             for i in range(PACK):
                 gather(a, i, 0, 256)
                 gather(a, i, 256, 512)
-                if i == 2 and a > 0:
-                    quantise(a - 1, 0, S)
-                if i == 2 and a == 1:
+                if (a, i) == (0, 3):
                     ws = keep.tile([P, PASSES, M], U8, name="ws", tag="early", align_bytes=64)
                     nc.gpsimd.memset(ws[:].rearrange("p a n -> p (a n)").bitcast(I32), 0)
                     for q in range(4):
@@ -129,43 +126,36 @@ def tile_list_heads_tm_res_kernel(tc, xT, w_words, w_scales, wgt, r, offs, out):
                             in_=w_scales[:, 4 * q : 4 * q + 4, :].rearrange("a q n -> q a n").bitcast(I32),
                         )
                 if i == 2 and a > 0:
+                    quantise(a - 1, 0, S)
                     for t in range(TOK_TILES):
                         multiply(ws, a - 1, t)
             interleave(a, 0, 256)
             interleave(a, 256, 512)
 
-        gather(last, 0, 0, 256)
-        gather(last, 0, 256, 512)
-        gather(last, 1, 0, 256)
-        gather(last, 1, 256, 512)
-        quantise(last - 1, 0, 256)
-        multiply(ws, last - 1, 0)
-        multiply(ws, last - 1, 1)
-        gather(last, 2, 0, 256)
-        quantise(last - 1, 256, 512)
-        multiply(ws, last - 1, 2)
-        multiply(ws, last - 1, 3)
-        gather(last, 2, 256, 512)
-        gather(last, 3, 0, 128)
-        interleave(last, 0, 128)
-        gather(last, 3, 128, 256)
-        interleave(last, 128, 256)
-        gather(last, 3, 256, 384)
-        interleave(last, 256, 384)
+        for i in range(PACK - 1):
+            gather(last, i, 0, 256)
+            gather(last, i, 256, 512)
+            if i == 2:
+                quantise(last - 1, 0, S)
+                for t in range(TOK_TILES):
+                    multiply(ws, last - 1, t)
+        gather(last, 3, 0, 256)
+        interleave(last, 0, 256)
         gather(last, 3, 384, 512)
-        quantise(last, 0, 128)
-        multiply(ws, last, 0)
+        gather(last, 3, 256, 384)
         nc.vector.tensor_copy(
             out=grouped[last][:, 384:512, :].rearrange("p (c l) i -> p c i l", l=4),
             in_=picked[last][:, :, 384:512].rearrange("p i (c l) -> p c i l", l=4),
         )
-        quantise(last, 128, 256)
+        interleave(last, 256, 384)
+        quantise(last, 0, 256)
+        multiply(ws, last, 0)
         multiply(ws, last, 1)
-        finish(0)
-        quantise(last, 256, 384)
-        multiply(ws, last, 2)
         quantise(last, 384, 512)
         multiply(ws, last, 3)
+        quantise(last, 256, 384)
+        multiply(ws, last, 2)
+        finish(0)
         finish(1)
-        finish(2)
         finish(3)
+        finish(2)

from contextlib import ExitStack

import concourse.mybir as mybir

K, M, T, S = 2048, 512, 1024, 512
FLOPS = 2 * K * M * S

F32 = mybir.dt.float32
BF16 = mybir.dt.bfloat16
I32 = mybir.dt.int32
U32 = mybir.dt.uint32
U16 = mybir.dt.uint16
U8 = mybir.dt.uint8
E4M3X4 = mybir.dt.float8_e4m3fn_x4
E2M1X4 = mybir.dt.float4_e2m1fn_x4
MULT = mybir.AluOpType.mult
ADD = mybir.AluOpType.add

P = 128
PACK = 4
K_PASS = P * PACK
PASSES = K // K_PASS
TOK = 128
TOK_TILES = S // TOK
PER_COL = 16


def tile_list_heads_tm_res_kernel(tc, xT, w_words, w_scales, wgt, r, offs, out):
    nc = tc.nc
    with ExitStack() as ctx:
        lists = ctx.enter_context(tc.tile_pool(name="lists", bufs=1))
        keep = ctx.enter_context(tc.tile_pool(name="keep", bufs=1))
        psum = ctx.enter_context(tc.psum_pool(name="psum", bufs=1))

        offsets = lists.tile([P, S // PER_COL], U16, name="offsets")
        x = [
            [
                keep.tile([P, T], F32, name=f"x{a}_{i}", tag="early" if (a, i) == (0, 2) else f"x{a}_{i}", align_bytes=64)
                for i in range(PACK)
            ]
            for a in range(PASSES)
        ]
        wg = [keep.tile([P, 256], F32, name=f"wg{h}") for h in range(2)]
        picked = [keep.tile([P, PACK, S], F32, name=f"picked{a}", align_bytes=64) for a in range(PASSES)]
        grouped = [keep.tile([P, S, PACK], BF16, name=f"grouped{a}", align_bytes=64) for a in range(PASSES)]
        codes = [keep.tile([P, S], U32, name=f"codes{a}", align_bytes=64) for a in range(PASSES)]
        scales = [keep.tile([P, S], U8, name=f"scales{a}", align_bytes=64) for a in range(PASSES)]
        ww = keep.tile([P, PASSES, 2 * M], U8, name="ww", align_bytes=64)
        res = [keep.tile([P, M], F32, name=f"res{t}") for t in range(TOK_TILES)]
        done = [keep.tile([P, M], F32, name=f"done{t}") for t in range(TOK_TILES)]
        acc = [psum.tile([P, M], F32, name=f"acc{t}") for t in range(TOK_TILES)]

        def load_x(a, i):
            rows = xT[a * K_PASS : (a + 1) * K_PASS, :].rearrange("(p i) t -> p i t", i=PACK)
            nc.sync.dma_start(out=x[a][i][:], in_=rows[:, i, :])

        def gather(a, i, lo, hi):
            half = lo // 256
            nc.vector.tensor_tensor(
                picked[a][:, i, lo:hi],
                x[a][i][:].indirect(offsets[:, lo // PER_COL : hi // PER_COL]),
                wg[half][:, lo - 256 * half : hi - 256 * half],
                MULT,
            )

        def interleave(a, lo, hi):
            nc.scalar.copy(
                out=grouped[a][:, lo:hi, :].rearrange("p (c l) i -> p c i l", l=4),
                in_=picked[a][:, :, lo:hi].rearrange("p i (c l) -> p c i l", l=4),
            )

        def quantise(a, lo, hi):
            nc.vector.quantize_mx(
                out=codes[a][:, lo:hi].bitcast(E4M3X4),
                scales=scales[a][:, lo:hi],
                in_=grouped[a][:, lo:hi, :].rearrange("p j i -> p (j i)"),
            )

        def multiply(ws, a, t):
            cols = slice(t * TOK, (t + 1) * TOK)
            nc.tensor.matmul_mx(
                out=acc[t][:],
                lhsT=codes[a][:, cols].bitcast(E4M3X4),
                lhsT_scale=scales[a][:, cols],
                rhs=ww[:, a, :].bitcast(E2M1X4),
                rhs_scale=ws[:, a, :],
                start=(a == 0),
                stop=(a == PASSES - 1),
            )

        def finish(t):
            rows = slice(t * TOK, (t + 1) * TOK)
            nc.vector.tensor_tensor(done[t][:], acc[t][:], res[t][:], ADD)
            nc.sync.dma_start(out=out[rows, :], in_=done[t][:])

        nc.sync.dma_start(offsets[:], offs)
        nc.scalar.dma_start(out=wg[0][:], in_=wgt[:, 0:256])
        load_x(0, 0)
        nc.sync.dma_start(out=wg[1][:], in_=wgt[:, 256:512])
        for i in range(1, PACK):
            load_x(0, i)
        for i in range(PACK):
            load_x(1, i)
        nc.sync.dma_start(
            out=ww[:].rearrange("p a n -> p (a n)").bitcast(I32).rearrange("p (a n) -> p a n", a=PASSES),
            in_=w_words.rearrange("a p n -> p a n").bitcast(I32),
        )
        for a in range(2, PASSES):
            for i in range(PACK):
                load_x(a, i)
        for t in range(TOK_TILES):
            nc.sync.dma_start(out=res[t][:], in_=r[t * TOK : (t + 1) * TOK, :])

        last = PASSES - 1
        ws = None
        for a in range(last):
            for i in range(PACK):
                gather(a, i, 0, 256)
                gather(a, i, 256, 512)
                if (a, i) == (0, 3):
                    ws = keep.tile([P, PASSES, M], U8, name="ws", tag="early", align_bytes=64)
                    nc.gpsimd.memset(ws[:].rearrange("p a n -> p (a n)").bitcast(I32), 0)
                    for q in range(4):
                        nc.scalar.dma_start(
                            out=ws[32 * q : 32 * q + 4, :, :].bitcast(I32),
                            in_=w_scales[:, 4 * q : 4 * q + 4, :].rearrange("a q n -> q a n").bitcast(I32),
                        )
                if i == 2 and a > 0:
                    quantise(a - 1, 0, S)
                    for t in range(TOK_TILES):
                        multiply(ws, a - 1, t)
            interleave(a, 0, 256)
            interleave(a, 256, 512)

        for i in range(PACK - 1):
            gather(last, i, 0, 256)
            gather(last, i, 256, 512)
            if i == 2:
                quantise(last - 1, 0, S)
                for t in range(TOK_TILES):
                    multiply(ws, last - 1, t)
        gather(last, 3, 0, 256)
        interleave(last, 0, 256)
        gather(last, 3, 384, 512)
        gather(last, 3, 256, 384)
        nc.vector.tensor_copy(
            out=grouped[last][:, 384:512, :].rearrange("p (c l) i -> p c i l", l=4),
            in_=picked[last][:, :, 384:512].rearrange("p i (c l) -> p c i l", l=4),
        )
        interleave(last, 256, 384)
        quantise(last, 0, 256)
        multiply(ws, last, 0)
        multiply(ws, last, 1)
        quantise(last, 384, 512)
        multiply(ws, last, 3)
        quantise(last, 256, 384)
        multiply(ws, last, 2)
        finish(0)
        finish(1)
        finish(3)
        finish(2)
